import numpy as np
import ml_dtypes


def mxq(x, axis, fmt="e4m3"):
    dtype, down = {"e4m3": (ml_dtypes.float8_e4m3fn, 7), "e5m2": (ml_dtypes.float8_e5m2, 14)}[fmt]
    v = np.moveaxis(np.asarray(x, np.float32).astype(ml_dtypes.bfloat16).astype(np.float64), axis, -1)
    blocks = v.reshape(v.shape[:-1] + (-1, 32))
    amax = np.abs(blocks).max(-1, keepdims=True)
    byte = np.maximum(np.where(amax > 0, np.frexp(amax)[1] - 1 + 127, 0) - down, 1)
    scale = np.exp2(byte - 127.0)
    codes = (blocks / scale).astype(np.float32).astype(dtype).astype(np.float64)
    return np.moveaxis((codes * scale).reshape(v.shape), -1, axis)


WIDE = False


def mx_kscale(k):
    if not WIDE:
        return np.ones(k)
    levels = np.array([10, -10, 5, -5, 0])
    if k % 512:
        return np.exp2(np.random.permutation(np.resize(levels, k // 32))).repeat(32)
    a = np.empty((k // 512, 16))
    for p in range(k // 512):
        a[p, :8] = np.random.permutation(np.resize(levels, 8))
        for g in range(8):
            far = levels[np.abs(levels - a[p, g]) >= 10]
            a[p, g + 8] = far[np.random.randint(len(far))]
    return np.exp2(a.ravel()).repeat(32)


def f64(x):
    return np.asarray(x).astype(np.float64)


def striped8(idx):
    return np.asarray(idx).reshape(8, -1, 16).transpose(0, 2, 1).reshape(128, -1).astype(np.uint16)


def unstriped8(offs):
    return offs.reshape(8, 16, -1).transpose(0, 2, 1).reshape(8, -1).astype(np.int64)


def pick8(x, idx, run):
    r = np.arange(len(x))
    return x[r[:, None], idx[r % (8 * run) // run]]


E2M1 = np.array([0.0, 0.5, 1.0, 1.5, 2.0, 3.0, 4.0, 6.0, -0.0, -0.5, -1.0, -1.5, -2.0, -3.0, -4.0, -6.0])


def pack_weight(w, fmt):
    k, n = w.shape
    w = f64(np.asarray(w, np.float32).astype(ml_dtypes.bfloat16)).reshape(k // 32, 32, n)
    amax = np.abs(w).max(1)
    if fmt == "e4m3":
        byte = np.frexp(amax)[1] - 1 + 127 - 7
    else:
        mant, ex = np.frexp(amax / 6.0)
        byte = np.where(mant > 0.5, ex, ex - 1) + 127
    byte = np.clip(np.where(amax > 0, byte, 1), 1, 254)
    scaled = (w * np.exp2(127.0 - byte)[:, None, :]).reshape(k, n).astype(np.float32)
    by_word = np.ascontiguousarray(scaled.reshape(k // 512, 128, 4, n).transpose(0, 1, 3, 2))
    if fmt == "e4m3":
        words = by_word.astype(ml_dtypes.float8_e4m3fn).view(np.uint8)
    else:
        c = by_word.astype(ml_dtypes.float4_e2m1fn).view(np.uint8) & 0xF
        words = (c[..., 0::2] | (c[..., 1::2] << 4)).reshape(k // 512, 128, 2 * n)
    return np.ascontiguousarray(words), np.ascontiguousarray(byte.astype(np.uint8).reshape(k // 512, 16, n))


def unpack_weight(words, scales, fmt):
    g, _, n = scales.shape
    words = np.ascontiguousarray(words).reshape(g, 128, n, -1)
    if fmt == "e4m3":
        vals = words.view(ml_dtypes.float8_e4m3fn).astype(np.float64)
    else:
        nib = np.empty((g, 128, n, 4), np.uint8)
        nib[..., 0::2] = words & 0xF
        nib[..., 1::2] = words >> 4
        vals = E2M1[nib]
    vals = vals * np.repeat(np.exp2(scales.astype(np.float64) - 127.0), 8, axis=1)[..., None]
    return vals.transpose(0, 1, 3, 2).reshape(g * 512, n)


D, T, U, I, Q = 512, 1024, 1024, 512, 128


def setup_inputs():
    n = np.random.standard_normal
    idx = np.stack([np.random.permutation(T)[:I] for _ in range(8)])
    idx2 = np.stack([np.random.permutation(T)[:I] for _ in range(8)])
    idx3 = np.stack([np.random.permutation(U)[:I] for _ in range(8)])
    idx4 = np.stack([np.random.permutation(U)[:I] for _ in range(8)])
    idx5 = np.stack([np.random.permutation(T)[:I] for _ in range(8)])
    fd = mx_kscale(D)
    cachep = pack_weight(n((D, T)) / fd[:, None], "e2m1")
    draftp = pack_weight(n((D, U)) / fd[:, None], "e4m3")
    return {
        "query": (n((D, Q)) * 1.0 / np.sqrt(D) * fd[:, None]).astype(np.float32),
        "cache_words": cachep[0],
        "cache_scales": cachep[1],
        "draft_words": draftp[0],
        "draft_scales": draftp[1],
        "offs": striped8(idx),
        "offs2": striped8(idx2),
        "offs3": striped8(idx3),
        "offs4": striped8(idx4),
        "offs5": striped8(idx5),
    }


def reference(query, cache_words, cache_scales, draft_words, draft_scales, offs, offs2, offs3, offs4, offs5):
    idx = unstriped8(offs)
    idx2 = unstriped8(offs2)
    idx3 = unstriped8(offs3)
    idx4 = unstriped8(offs4)
    idx5 = unstriped8(offs5)
    cacheu = unpack_weight(cache_words, cache_scales, "e2m1")
    draftu = unpack_weight(draft_words, draft_scales, "e4m3")
    queryq = mxq(f64(query), 0, "e4m3")
    a = queryq.T @ cacheu
    b = queryq.T @ draftu
    lo1 = np.minimum(pick8(a, idx, 16), pick8(a, idx2, 16))
    hi1 = np.maximum(pick8(a, idx, 16), pick8(a, idx2, 16))
    f1 = np.zeros((Q, U))
    f1[np.arange(Q)[:, None], idx3[np.arange(Q) % 128 // 16]] = lo1
    bb = np.maximum(b, f1)
    v = pick8(bb, idx4, 16) - hi1
    f2 = np.zeros((Q, T))
    f2[np.arange(Q)[:, None], idx5[np.arange(Q) % 128 // 16]] = v
    aa = a + f2
    y = pick8(aa, idx2, 16)
    return y

@@ -1,0 +1,147 @@
+from contextlib import ExitStack
+
+import concourse.mybir as mybir
+
+D, T, U, I, Q = 512, 1024, 1024, 512, 128
+FLOPS = 2 * Q * D * (T + U)
+
+F32 = mybir.dt.float32
+BF16 = mybir.dt.bfloat16
+I32 = mybir.dt.int32
+U32 = mybir.dt.uint32
+U16 = mybir.dt.uint16
+U8 = mybir.dt.uint8
+FP8X4 = mybir.dt.float8_e4m3fn_x4
+FP4X4 = mybir.dt.float4_e2m1fn_x4
+ALU = mybir.AluOpType
+COPY = mybir.ActivationFunctionType.Copy
+
+P = 128
+PACK = 4
+HALF = I // 2
+HALF_COLS = HALF // 16
+
+
+def tile_attend_evictlow_two_kernel(
+    tc, query, cache_words, cache_scales, draft_words, draft_scales, offs, offs2, offs3, offs4, offs5, out
+):
+    nc = tc.nc
+    with ExitStack() as ctx:
+        sb = ctx.enter_context(tc.tile_pool(name="sb", bufs=1))
+        ps = ctx.enter_context(tc.psum_pool(name="ps", bufs=1))
+
+        c_scale = sb.tile([P, T], U8, align_bytes=64)
+        d_scale = sb.tile([P, U], U8, align_bytes=64)
+        f1 = sb.tile([P, U], F32)
+        f2 = sb.tile([P, T], F32)
+        nc.vector.memset(c_scale[:].bitcast(I32), 0)
+        nc.vector.memset(d_scale[:].bitcast(I32), 0)
+        nc.vector.memset(f1[:], 0.0)
+        nc.vector.memset(f2[:], 0.0)
+
+        def load_scales(plane, rows):
+            for quad in range(4):
+                nc.sync.dma_start(
+                    out=plane[32 * quad : 32 * quad + 4, :].bitcast(I32),
+                    in_=rows[0, 4 * quad : 4 * quad + 4, :].bitcast(I32),
+                )
+
+        def load_list(name, src):
+            t = sb.tile([P, I // 16], U16, name=name)
+            nc.sync.dma_start(t[:], src)
+            return t
+
+        q_raw = sb.tile([P, PACK, Q], F32)
+        nc.sync.dma_start(out=q_raw[:], in_=query.rearrange("(p j) q -> p j q", j=PACK))
+        c_words = sb.tile([P, 2 * T], U8, align_bytes=64)
+        nc.sync.dma_start(out=c_words[:].bitcast(I32), in_=cache_words[0].bitcast(I32))
+        load_scales(c_scale, cache_scales)
+        l1 = load_list("l1", offs)
+        l2 = load_list("l2", offs2)
+        l3 = load_list("l3", offs3)
+        d_words = sb.tile([P, U], I32, align_bytes=64)
+        nc.sync.dma_start(out=d_words[:], in_=draft_words[0].rearrange("p n t -> p (n t)").bitcast(I32))
+        load_scales(d_scale, draft_scales)
+        l4 = load_list("l4", offs4)
+        l5 = load_list("l5", offs5)
+
+        q_bf = sb.tile([P, Q, PACK], BF16, align_bytes=64)
+        nc.vector.tensor_copy(out=q_bf[:], in_=q_raw[:].rearrange("p j q -> p q j"))
+        q_codes = sb.tile([P, Q], U32, align_bytes=64)
+        q_scale = sb.tile([P, Q], U8, align_bytes=64)
+        nc.vector.quantize_mx(
+            out=q_codes[:].bitcast(FP8X4), scales=q_scale[:], in_=q_bf[:].rearrange("p q j -> p (q j)")
+        )
+
+        a = sb.tile([P, T], F32)
+        for n in range(4):
+            cols = slice(256 * n, 256 * (n + 1))
+            acc = ps.tile([P, 256], F32, name=f"a_ps{n}")
+            nc.tensor.matmul_mx(
+                out=acc[:],
+                lhsT=q_codes[:].bitcast(FP8X4),
+                lhsT_scale=q_scale[:],
+                rhs=c_words[:, 512 * n : 512 * (n + 1)].bitcast(FP4X4),
+                rhs_scale=c_scale[:, cols],
+                start=True,
+                stop=True,
+            )
+            if n % 2 == 0:
+                nc.vector.tensor_copy(out=a[:, cols], in_=acc[:])
+            else:
+                nc.scalar.copy(out=a[:, cols], in_=acc[:])
+
+        b_ps = []
+        for n in range(2):
+            cols = slice(512 * n, 512 * (n + 1))
+            acc = ps.tile([P, 512], F32, name=f"b_ps{n}")
+            nc.tensor.matmul_mx(
+                out=acc[:],
+                lhsT=q_codes[:].bitcast(FP8X4),
+                lhsT_scale=q_scale[:],
+                rhs=d_words[:, cols].bitcast(FP8X4),
+                rhs_scale=d_scale[:, cols],
+                start=True,
+                stop=True,
+            )
+            b_ps.append(acc)
+
+        def slots(h):
+            return slice(HALF * h, HALF * (h + 1))
+
+        def entries(h):
+            return slice(HALF_COLS * h, HALF_COLS * (h + 1))
+
+        g1 = sb.tile([P, I], F32)
+        g2 = sb.tile([P, I], F32)
+        lo = sb.tile([P, I], F32)
+        hi = sb.tile([P, I], F32)
+        nc.vector.tensor_copy(g1[:, slots(0)], a[:].indirect(l1[:, entries(0)]))
+        nc.scalar.activation(g2[:, slots(0)], a[:].indirect(l2[:, entries(0)]), COPY)
+        nc.vector.tensor_tensor(lo[:, slots(0)], g1[:, slots(0)], g2[:, slots(0)], ALU.min)
+        nc.scalar.activation(f1[:].indirect(l3[:, entries(0)]), lo[:, slots(0)], COPY)
+        nc.vector.tensor_copy(g1[:, slots(1)], a[:].indirect(l1[:, entries(1)]))
+        nc.vector.tensor_copy(g2[:, slots(1)], a[:].indirect(l2[:, entries(1)]))
+        nc.vector.tensor_tensor(lo[:, slots(1)], g1[:, slots(1)], g2[:, slots(1)], ALU.min)
+        nc.scalar.activation(f1[:].indirect(l3[:, entries(1)]), lo[:, slots(1)], COPY)
+        nc.vector.tensor_tensor(hi[:], g1[:], g2[:], ALU.max)
+
+        bb = sb.tile([P, U], F32)
+        for n in range(2):
+            cols = slice(512 * n, 512 * (n + 1))
+            nc.vector.tensor_tensor(bb[:, cols], b_ps[n][:], f1[:, cols], ALU.max)
+
+        v = sb.tile([P, I], F32)
+        for h in range(2):
+            nc.vector.tensor_tensor(v[:, slots(h)], bb[:].indirect(l4[:, entries(h)]), hi[:, slots(h)], ALU.subtract)
+            nc.scalar.activation(f2[:].indirect(l5[:, entries(h)]), v[:, slots(h)], COPY)
+
+        aa = sb.tile([P, T], F32)
+        nc.vector.tensor_tensor(aa[:], a[:], f2[:], ALU.add)
+
+        y0 = sb.tile([P, HALF], F32)
+        y1 = sb.tile([P, HALF], F32)
+        nc.vector.tensor_copy(y0[:], aa[:].indirect(l2[:, entries(0)]))
+        nc.scalar.activation(y1[:], aa[:].indirect(l2[:, entries(1)]), COPY)
+        nc.sync.dma_start(out=out[:, slots(0)], in_=y0[:])
+        nc.scalar.dma_start(out=out[:, slots(1)], in_=y1[:])

@@ -18,8 +18,36 @@ COPY = mybir.ActivationFunctionType.Copy
 
 P = 128
 PACK = 4
+QUADRANT = 32
+SCALE_ROWS = 4
+GROUP = 16
 HALF = I // 2
-HALF_COLS = HALF // 16
+BANK = 512
+
+ROWS_ON_VECTOR = 80
+A_EDGES = (0, 256, 512, 768, 896, 1024)
+
+
+def slots(h):
+    return slice(HALF * h, HALF * (h + 1))
+
+
+def entries(h):
+    return slice(HALF // GROUP * h, HALF // GROUP * (h + 1))
+
+
+def load_scales(nc, scale_tile, rows):
+    for n in range(P // QUADRANT):
+        nc.sync.dma_start(
+            out=scale_tile[QUADRANT * n : QUADRANT * n + SCALE_ROWS, :].bitcast(I32),
+            in_=rows[0, SCALE_ROWS * n : SCALE_ROWS * (n + 1), :].bitcast(I32),
+        )
+
+
+def load_list(nc, pool, name, src):
+    offsets = pool.tile([P, I // GROUP], U16, name=name)
+    nc.sync.dma_start(offsets[:], src)
+    return offsets
 
 
 def tile_attend_evictlow_two_kernel(
@@ -33,115 +61,95 @@ def tile_attend_evictlow_two_kernel(
         c_scale = sb.tile([P, T], U8, align_bytes=64)
         d_scale = sb.tile([P, U], U8, align_bytes=64)
         f1 = sb.tile([P, U], F32)
-        f2 = sb.tile([P, T], F32)
         nc.vector.memset(c_scale[:].bitcast(I32), 0)
         nc.vector.memset(d_scale[:].bitcast(I32), 0)
         nc.vector.memset(f1[:], 0.0)
-        nc.vector.memset(f2[:], 0.0)
-
-        def load_scales(plane, rows):
-            for quad in range(4):
-                nc.sync.dma_start(
-                    out=plane[32 * quad : 32 * quad + 4, :].bitcast(I32),
-                    in_=rows[0, 4 * quad : 4 * quad + 4, :].bitcast(I32),
-                )
-
-        def load_list(name, src):
-            t = sb.tile([P, I // 16], U16, name=name)
-            nc.sync.dma_start(t[:], src)
-            return t
 
         q_raw = sb.tile([P, PACK, Q], F32)
-        nc.sync.dma_start(out=q_raw[:], in_=query.rearrange("(p j) q -> p j q", j=PACK))
+        nc.sync.dma_start(out=q_raw[:], in_=query.rearrange("(p t) q -> p t q", t=PACK))
         c_words = sb.tile([P, 2 * T], U8, align_bytes=64)
         nc.sync.dma_start(out=c_words[:].bitcast(I32), in_=cache_words[0].bitcast(I32))
-        load_scales(c_scale, cache_scales)
-        l1 = load_list("l1", offs)
-        l2 = load_list("l2", offs2)
-        l3 = load_list("l3", offs3)
+        load_scales(nc, c_scale, cache_scales)
+        idx1 = load_list(nc, sb, "idx1", offs)
+        idx2 = load_list(nc, sb, "idx2", offs2)
+        idx3 = load_list(nc, sb, "idx3", offs3)
         d_words = sb.tile([P, U], I32, align_bytes=64)
         nc.sync.dma_start(out=d_words[:], in_=draft_words[0].rearrange("p n t -> p (n t)").bitcast(I32))
-        load_scales(d_scale, draft_scales)
-        l4 = load_list("l4", offs4)
-        l5 = load_list("l5", offs5)
+        load_scales(nc, d_scale, draft_scales)
+        idx4 = load_list(nc, sb, "idx4", offs4)
+        idx5 = load_list(nc, sb, "idx5", offs5)
 
         q_bf = sb.tile([P, Q, PACK], BF16, align_bytes=64)
-        nc.vector.tensor_copy(out=q_bf[:], in_=q_raw[:].rearrange("p j q -> p q j"))
+        q_by_row = q_raw[:].rearrange("p t q -> p q t")
+        nc.vector.tensor_copy(out=q_bf[:, :ROWS_ON_VECTOR, :], in_=q_by_row[:, :ROWS_ON_VECTOR, :])
+        nc.scalar.copy(out=q_bf[:, ROWS_ON_VECTOR:, :], in_=q_by_row[:, ROWS_ON_VECTOR:, :])
         q_codes = sb.tile([P, Q], U32, align_bytes=64)
         q_scale = sb.tile([P, Q], U8, align_bytes=64)
         nc.vector.quantize_mx(
-            out=q_codes[:].bitcast(FP8X4), scales=q_scale[:], in_=q_bf[:].rearrange("p q j -> p (q j)")
+            out=q_codes[:].bitcast(FP8X4), scales=q_scale[:], in_=q_bf[:].rearrange("p q t -> p (q t)")
         )
 
-        a = sb.tile([P, T], F32)
-        for n in range(4):
-            cols = slice(256 * n, 256 * (n + 1))
-            acc = ps.tile([P, 256], F32, name=f"a_ps{n}")
+        def scores(name, words, scales):
+            acc = ps.tile([Q, scales.shape[1]], F32, name=name)
             nc.tensor.matmul_mx(
                 out=acc[:],
                 lhsT=q_codes[:].bitcast(FP8X4),
                 lhsT_scale=q_scale[:],
-                rhs=c_words[:, 512 * n : 512 * (n + 1)].bitcast(FP4X4),
-                rhs_scale=c_scale[:, cols],
+                rhs=words,
+                rhs_scale=scales,
                 start=True,
                 stop=True,
             )
+            return acc
+
+        a = sb.tile([Q, T], F32)
+        for n, (first, last) in enumerate(zip(A_EDGES, A_EDGES[1:])):
+            acc = scores(f"a_ps{n}", c_words[:, 2 * first : 2 * last].bitcast(FP4X4), c_scale[:, first:last])
             if n % 2 == 0:
-                nc.vector.tensor_copy(out=a[:, cols], in_=acc[:])
+                nc.vector.tensor_copy(out=a[:, first:last], in_=acc[:])
             else:
-                nc.scalar.copy(out=a[:, cols], in_=acc[:])
+                nc.scalar.copy(out=a[:, first:last], in_=acc[:])
+        b_cols = [slice(first, first + BANK) for first in range(0, U, BANK)]
+        b_ps = [
+            scores(f"b_ps{n}", d_words[:, cols].bitcast(FP8X4), d_scale[:, cols]) for n, cols in enumerate(b_cols)
+        ]
 
-        b_ps = []
-        for n in range(2):
-            cols = slice(512 * n, 512 * (n + 1))
-            acc = ps.tile([P, 512], F32, name=f"b_ps{n}")
-            nc.tensor.matmul_mx(
-                out=acc[:],
-                lhsT=q_codes[:].bitcast(FP8X4),
-                lhsT_scale=q_scale[:],
-                rhs=d_words[:, cols].bitcast(FP8X4),
-                rhs_scale=d_scale[:, cols],
-                start=True,
-                stop=True,
-            )
-            b_ps.append(acc)
-
-        def slots(h):
-            return slice(HALF * h, HALF * (h + 1))
-
-        def entries(h):
-            return slice(HALF_COLS * h, HALF_COLS * (h + 1))
-
-        g1 = sb.tile([P, I], F32)
-        g2 = sb.tile([P, I], F32)
-        lo = sb.tile([P, I], F32)
-        hi = sb.tile([P, I], F32)
-        nc.vector.tensor_copy(g1[:, slots(0)], a[:].indirect(l1[:, entries(0)]))
-        nc.scalar.activation(g2[:, slots(0)], a[:].indirect(l2[:, entries(0)]), COPY)
-        nc.vector.tensor_tensor(lo[:, slots(0)], g1[:, slots(0)], g2[:, slots(0)], ALU.min)
-        nc.scalar.activation(f1[:].indirect(l3[:, entries(0)]), lo[:, slots(0)], COPY)
-        nc.vector.tensor_copy(g1[:, slots(1)], a[:].indirect(l1[:, entries(1)]))
-        nc.vector.tensor_copy(g2[:, slots(1)], a[:].indirect(l2[:, entries(1)]))
-        nc.vector.tensor_tensor(lo[:, slots(1)], g1[:, slots(1)], g2[:, slots(1)], ALU.min)
-        nc.scalar.activation(f1[:].indirect(l3[:, entries(1)]), lo[:, slots(1)], COPY)
-        nc.vector.tensor_tensor(hi[:], g1[:], g2[:], ALU.max)
-
-        bb = sb.tile([P, U], F32)
-        for n in range(2):
-            cols = slice(512 * n, 512 * (n + 1))
-            nc.vector.tensor_tensor(bb[:, cols], b_ps[n][:], f1[:, cols], ALU.max)
-
-        v = sb.tile([P, I], F32)
+        a_idx2 = sb.tile([Q, I], F32, tag="a_idx2")
+        lo = sb.tile([Q, I], F32)
+        hi = sb.tile([Q, I], F32)
         for h in range(2):
-            nc.vector.tensor_tensor(v[:, slots(h)], bb[:].indirect(l4[:, entries(h)]), hi[:, slots(h)], ALU.subtract)
-            nc.scalar.activation(f2[:].indirect(l5[:, entries(h)]), v[:, slots(h)], COPY)
+            a_idx1 = sb.tile([Q, HALF], F32, tag="a_idx1")
+            nc.vector.tensor_copy(a_idx1[:], a[:].indirect(idx1[:, entries(h)]))
+            nc.scalar.activation(a_idx2[:, slots(h)], a[:].indirect(idx2[:, entries(h)]), COPY)
+            nc.vector.tensor_tensor(lo[:, slots(h)], a_idx1[:], a_idx2[:, slots(h)], ALU.min)
+            nc.vector.tensor_tensor(hi[:, slots(h)], a_idx1[:], a_idx2[:, slots(h)], ALU.max)
+        for h in range(2):
+            nc.scalar.activation(f1[:].indirect(idx3[:, entries(h)]), lo[:, slots(h)], COPY)
 
-        aa = sb.tile([P, T], F32)
-        nc.vector.tensor_tensor(aa[:], a[:], f2[:], ALU.add)
+        f2_first = sb.tile([Q, T], F32, tag="a_idx2")
+        f2_second = sb.tile([Q, T], F32, tag="a_idx1")
+        nc.gpsimd.memset(f2_first[:], 0.0)
+        nc.gpsimd.memset(f2_second[:], 0.0)
 
-        y0 = sb.tile([P, HALF], F32)
-        y1 = sb.tile([P, HALF], F32)
-        nc.vector.tensor_copy(y0[:], aa[:].indirect(l2[:, entries(0)]))
-        nc.scalar.activation(y1[:], aa[:].indirect(l2[:, entries(1)]), COPY)
-        nc.sync.dma_start(out=out[:, slots(0)], in_=y0[:])
-        nc.scalar.dma_start(out=out[:, slots(1)], in_=y1[:])
+        bb = sb.tile([Q, U], F32)
+        for cols, acc in zip(b_cols, b_ps):
+            nc.vector.tensor_tensor(bb[:, cols], acc[:], f1[:, cols], ALU.max)
+
+        v = sb.tile([Q, I], F32)
+        for h, f2_half in enumerate((f2_first, f2_second)):
+            nc.vector.tensor_tensor(
+                v[:, slots(h)], bb[:].indirect(idx4[:, entries(h)]), hi[:, slots(h)], ALU.subtract
+            )
+            nc.scalar.activation(f2_half[:].indirect(idx5[:, entries(h)]), v[:, slots(h)], COPY)
+
+        aa = sb.tile([Q, T], F32)
+        a_plus_first = sb.tile([Q, T], F32)
+        nc.vector.tensor_tensor(a_plus_first[:], a[:], f2_first[:], ALU.add)
+        nc.vector.tensor_tensor(aa[:], a_plus_first[:], f2_second[:], ALU.add)
+
+        y_first = sb.tile([Q, HALF], F32)
+        y_second = sb.tile([Q, HALF], F32)
+        nc.vector.tensor_copy(y_first[:], aa[:].indirect(idx2[:, entries(0)]))
+        nc.scalar.activation(y_second[:], aa[:].indirect(idx2[:, entries(1)]), COPY)
+        nc.sync.dma_start(out=out[:, slots(0)], in_=y_first[:])
+        nc.scalar.dma_start(out=out[:, slots(1)], in_=y_second[:])

@@ -68,9 +68,10 @@ def tile_attend_evictlow_two_kernel(
         q_raw = sb.tile([P, PACK, Q], F32)
         nc.sync.dma_start(out=q_raw[:], in_=query.rearrange("(p t) q -> p t q", t=PACK))
         c_words = sb.tile([P, 2 * T], U8, align_bytes=64)
-        nc.sync.dma_start(out=c_words[:].bitcast(I32), in_=cache_words[0].bitcast(I32))
-        load_scales(nc, c_scale, cache_scales)
+        nc.sync.dma_start(out=c_words[:, :T].bitcast(I32), in_=cache_words[0, :, :T].bitcast(I32))
         idx1 = load_list(nc, sb, "idx1", offs)
+        load_scales(nc, c_scale, cache_scales)
+        nc.sync.dma_start(out=c_words[:, T:].bitcast(I32), in_=cache_words[0, :, T:].bitcast(I32))
         idx2 = load_list(nc, sb, "idx2", offs2)
         idx3 = load_list(nc, sb, "idx3", offs3)
         d_words = sb.tile([P, U], I32, align_bytes=64)

from contextlib import ExitStack

import concourse.mybir as mybir

D, T, U, I, Q = 512, 1024, 1024, 512, 128
FLOPS = 2 * Q * D * (T + U)

F32 = mybir.dt.float32
BF16 = mybir.dt.bfloat16
I32 = mybir.dt.int32
U32 = mybir.dt.uint32
U16 = mybir.dt.uint16
U8 = mybir.dt.uint8
FP8X4 = mybir.dt.float8_e4m3fn_x4
FP4X4 = mybir.dt.float4_e2m1fn_x4
ALU = mybir.AluOpType
COPY = mybir.ActivationFunctionType.Copy

P = 128
PACK = 4
QUADRANT = 32
SCALE_ROWS = 4
GROUP = 16
HALF = I // 2
BANK = 512

ROWS_ON_VECTOR = 80
A_EDGES = (0, 256, 512, 768, 896, 1024)


def slots(h):
    return slice(HALF * h, HALF * (h + 1))


def entries(h):
    return slice(HALF // GROUP * h, HALF // GROUP * (h + 1))


def load_scales(nc, scale_tile, rows):
    for n in range(P // QUADRANT):
        nc.sync.dma_start(
            out=scale_tile[QUADRANT * n : QUADRANT * n + SCALE_ROWS, :].bitcast(I32),
            in_=rows[0, SCALE_ROWS * n : SCALE_ROWS * (n + 1), :].bitcast(I32),
        )


def load_list(nc, pool, name, src):
    offsets = pool.tile([P, I // GROUP], U16, name=name)
    nc.sync.dma_start(offsets[:], src)
    return offsets


def tile_attend_evictlow_two_kernel(
    tc, query, cache_words, cache_scales, draft_words, draft_scales, offs, offs2, offs3, offs4, offs5, out
):
    nc = tc.nc
    with ExitStack() as ctx:
        sb = ctx.enter_context(tc.tile_pool(name="sb", bufs=1))
        ps = ctx.enter_context(tc.psum_pool(name="ps", bufs=1))

        c_scale = sb.tile([P, T], U8, align_bytes=64)
        d_scale = sb.tile([P, U], U8, align_bytes=64)
        f1 = sb.tile([P, U], F32)
        nc.vector.memset(c_scale[:].bitcast(I32), 0)
        nc.vector.memset(d_scale[:].bitcast(I32), 0)
        nc.vector.memset(f1[:], 0.0)

        q_raw = sb.tile([P, PACK, Q], F32)
        nc.sync.dma_start(out=q_raw[:], in_=query.rearrange("(p t) q -> p t q", t=PACK))
        c_words = sb.tile([P, 2 * T], U8, align_bytes=64)
        nc.sync.dma_start(out=c_words[:, :T].bitcast(I32), in_=cache_words[0, :, :T].bitcast(I32))
        idx1 = load_list(nc, sb, "idx1", offs)
        load_scales(nc, c_scale, cache_scales)
        nc.sync.dma_start(out=c_words[:, T:].bitcast(I32), in_=cache_words[0, :, T:].bitcast(I32))
        idx2 = load_list(nc, sb, "idx2", offs2)
        idx3 = load_list(nc, sb, "idx3", offs3)
        d_words = sb.tile([P, U], I32, align_bytes=64)
        nc.sync.dma_start(out=d_words[:], in_=draft_words[0].rearrange("p n t -> p (n t)").bitcast(I32))
        load_scales(nc, d_scale, draft_scales)
        idx4 = load_list(nc, sb, "idx4", offs4)
        idx5 = load_list(nc, sb, "idx5", offs5)

        q_bf = sb.tile([P, Q, PACK], BF16, align_bytes=64)
        q_by_row = q_raw[:].rearrange("p t q -> p q t")
        nc.vector.tensor_copy(out=q_bf[:, :ROWS_ON_VECTOR, :], in_=q_by_row[:, :ROWS_ON_VECTOR, :])
        nc.scalar.copy(out=q_bf[:, ROWS_ON_VECTOR:, :], in_=q_by_row[:, ROWS_ON_VECTOR:, :])
        q_codes = sb.tile([P, Q], U32, align_bytes=64)
        q_scale = sb.tile([P, Q], U8, align_bytes=64)
        nc.vector.quantize_mx(
            out=q_codes[:].bitcast(FP8X4), scales=q_scale[:], in_=q_bf[:].rearrange("p q t -> p (q t)")
        )

        def scores(name, words, scales):
            acc = ps.tile([Q, scales.shape[1]], F32, name=name)
            nc.tensor.matmul_mx(
                out=acc[:],
                lhsT=q_codes[:].bitcast(FP8X4),
                lhsT_scale=q_scale[:],
                rhs=words,
                rhs_scale=scales,
                start=True,
                stop=True,
            )
            return acc

        a = sb.tile([Q, T], F32)
        for n, (first, last) in enumerate(zip(A_EDGES, A_EDGES[1:])):
            acc = scores(f"a_ps{n}", c_words[:, 2 * first : 2 * last].bitcast(FP4X4), c_scale[:, first:last])
            if n % 2 == 0:
                nc.vector.tensor_copy(out=a[:, first:last], in_=acc[:])
            else:
                nc.scalar.copy(out=a[:, first:last], in_=acc[:])
        b_cols = [slice(first, first + BANK) for first in range(0, U, BANK)]
        b_ps = [
            scores(f"b_ps{n}", d_words[:, cols].bitcast(FP8X4), d_scale[:, cols]) for n, cols in enumerate(b_cols)
        ]

        a_idx2 = sb.tile([Q, I], F32, tag="a_idx2")
        lo = sb.tile([Q, I], F32)
        hi = sb.tile([Q, I], F32)
        for h in range(2):
            a_idx1 = sb.tile([Q, HALF], F32, tag="a_idx1")
            nc.vector.tensor_copy(a_idx1[:], a[:].indirect(idx1[:, entries(h)]))
            nc.scalar.activation(a_idx2[:, slots(h)], a[:].indirect(idx2[:, entries(h)]), COPY)
            nc.vector.tensor_tensor(lo[:, slots(h)], a_idx1[:], a_idx2[:, slots(h)], ALU.min)
            nc.vector.tensor_tensor(hi[:, slots(h)], a_idx1[:], a_idx2[:, slots(h)], ALU.max)
        for h in range(2):
            nc.scalar.activation(f1[:].indirect(idx3[:, entries(h)]), lo[:, slots(h)], COPY)

        f2_first = sb.tile([Q, T], F32, tag="a_idx2")
        f2_second = sb.tile([Q, T], F32, tag="a_idx1")
        nc.gpsimd.memset(f2_first[:], 0.0)
        nc.gpsimd.memset(f2_second[:], 0.0)

        bb = sb.tile([Q, U], F32)
        for cols, acc in zip(b_cols, b_ps):
            nc.vector.tensor_tensor(bb[:, cols], acc[:], f1[:, cols], ALU.max)

        v = sb.tile([Q, I], F32)
        for h, f2_half in enumerate((f2_first, f2_second)):
            nc.vector.tensor_tensor(
                v[:, slots(h)], bb[:].indirect(idx4[:, entries(h)]), hi[:, slots(h)], ALU.subtract
            )
            nc.scalar.activation(f2_half[:].indirect(idx5[:, entries(h)]), v[:, slots(h)], COPY)

        aa = sb.tile([Q, T], F32)
        a_plus_first = sb.tile([Q, T], F32)
        nc.vector.tensor_tensor(a_plus_first[:], a[:], f2_first[:], ALU.add)
        nc.vector.tensor_tensor(aa[:], a_plus_first[:], f2_second[:], ALU.add)

        y_first = sb.tile([Q, HALF], F32)
        y_second = sb.tile([Q, HALF], F32)
        nc.vector.tensor_copy(y_first[:], aa[:].indirect(idx2[:, entries(0)]))
        nc.scalar.activation(y_second[:], aa[:].indirect(idx2[:, entries(1)]), COPY)
        nc.sync.dma_start(out=out[:, slots(0)], in_=y_first[:])
        nc.scalar.dma_start(out=out[:, slots(1)], in_=y_second[:])
